import numpy as np
import ml_dtypes


def mxq(x, axis, fmt="e4m3"):
    dtype, down = {"e4m3": (ml_dtypes.float8_e4m3fn, 7), "e5m2": (ml_dtypes.float8_e5m2, 14)}[fmt]
    v = np.moveaxis(np.asarray(x, np.float32).astype(ml_dtypes.bfloat16).astype(np.float64), axis, -1)
    blocks = v.reshape(v.shape[:-1] + (-1, 32))
    amax = np.abs(blocks).max(-1, keepdims=True)
    byte = np.maximum(np.where(amax > 0, np.frexp(amax)[1] - 1 + 127, 0) - down, 1)
    scale = np.exp2(byte - 127.0)
    codes = (blocks / scale).astype(np.float32).astype(dtype).astype(np.float64)
    return np.moveaxis((codes * scale).reshape(v.shape), -1, axis)


WIDE = False


def mx_kscale(k):
    if not WIDE:
        return np.ones(k)
    levels = np.array([10, -10, 5, -5, 0])
    if k % 512:
        return np.exp2(np.random.permutation(np.resize(levels, k // 32))).repeat(32)
    a = np.empty((k // 512, 16))
    for p in range(k // 512):
        a[p, :8] = np.random.permutation(np.resize(levels, 8))
        for g in range(8):
            far = levels[np.abs(levels - a[p, g]) >= 10]
            a[p, g + 8] = far[np.random.randint(len(far))]
    return np.exp2(a.ravel()).repeat(32)


def f64(x):
    return np.asarray(x).astype(np.float64)


def striped(idx):
    return np.tile(np.asarray(idx).reshape(-1, 16).T, (8, 1)).astype(np.uint16)


def unstriped(offs):
    return offs[:16].T.reshape(-1).astype(np.int64)


E2M1 = np.array([0.0, 0.5, 1.0, 1.5, 2.0, 3.0, 4.0, 6.0, -0.0, -0.5, -1.0, -1.5, -2.0, -3.0, -4.0, -6.0])


def pack_weight(w, fmt):
    k, n = w.shape
    w = f64(np.asarray(w, np.float32).astype(ml_dtypes.bfloat16)).reshape(k // 32, 32, n)
    amax = np.abs(w).max(1)
    if fmt == "e4m3":
        byte = np.frexp(amax)[1] - 1 + 127 - 7
    else:
        mant, ex = np.frexp(amax / 6.0)
        byte = np.where(mant > 0.5, ex, ex - 1) + 127
    byte = np.clip(np.where(amax > 0, byte, 1), 1, 254)
    scaled = (w * np.exp2(127.0 - byte)[:, None, :]).reshape(k, n).astype(np.float32)
    by_word = np.ascontiguousarray(scaled.reshape(k // 512, 128, 4, n).transpose(0, 1, 3, 2))
    if fmt == "e4m3":
        words = by_word.astype(ml_dtypes.float8_e4m3fn).view(np.uint8)
    else:
        c = by_word.astype(ml_dtypes.float4_e2m1fn).view(np.uint8) & 0xF
        words = (c[..., 0::2] | (c[..., 1::2] << 4)).reshape(k // 512, 128, 2 * n)
    return np.ascontiguousarray(words), np.ascontiguousarray(byte.astype(np.uint8).reshape(k // 512, 16, n))


def unpack_weight(words, scales, fmt):
    g, _, n = scales.shape
    words = np.ascontiguousarray(words).reshape(g, 128, n, -1)
    if fmt == "e4m3":
        vals = words.view(ml_dtypes.float8_e4m3fn).astype(np.float64)
    else:
        nib = np.empty((g, 128, n, 4), np.uint8)
        nib[..., 0::2] = words & 0xF
        nib[..., 1::2] = words >> 4
        vals = E2M1[nib]
    vals = vals * np.repeat(np.exp2(scales.astype(np.float64) - 127.0), 8, axis=1)[..., None]
    return vals.transpose(0, 1, 3, 2).reshape(g * 512, n)


def sigmoid(v):
    return 1.0 / (1.0 + np.exp(-v))


D, E, T, I, Q, U = 512, 512, 1024, 256, 512, 1024


def setup_inputs():
    n = np.random.standard_normal
    idx = np.random.permutation(T)[:I]
    idx4 = np.random.permutation(U)[:I]
    fd = mx_kscale(D)
    fe = mx_kscale(E)
    fq = mx_kscale(Q)
    keysp = pack_weight(n((D, T)) / fd[:, None], "e2m1")
    valsp = pack_weight(n((E, T)) / fe[:, None], "e2m1")
    return {
        "query": (n((D, Q)) * 0.8 / np.sqrt(D) * fd[:, None]).astype(np.float32),
        "keys_words": keysp[0],
        "keys_scales": keysp[1],
        "share": (np.random.uniform(0.2, 0.8, (Q, 1))).astype(np.float32),
        "gout": (n((E, Q)) * 1 / np.sqrt(E) * fe[:, None]).astype(np.float32),
        "vals_words": valsp[0],
        "vals_scales": valsp[1],
        "qs": (np.random.uniform(100.0, 400.0, (Q, 1)) * fq[:, None]).astype(np.float32),
        "qrows": (n((Q, D)) / fq[:, None]).astype(np.float32),
        "old": (n((D, U)) * 4.0).astype(np.float32),
        "fade": (np.random.uniform(0.5, 1.0, (1, U))).astype(np.float32),
        "offs": striped(idx),
        "offs4": striped(idx4),
    }


def reference(query, keys_words, keys_scales, share, gout, vals_words, vals_scales, qs, qrows, old, fade, offs, offs4):
    idx = unstriped(offs)
    idx4 = unstriped(offs4)
    keysu = unpack_weight(keys_words, keys_scales, "e2m1")
    valsu = unpack_weight(vals_words, vals_scales, "e2m1")
    queryq = mxq(f64(query), 0, "e4m3")
    keysidxg = keysu[:, idx]
    a = queryq.T @ keysidxg
    e0 = np.exp(a)
    s0 = sigmoid(a)
    p = e0 * f64(share) + s0 * (1.0 - f64(share)) * 3.0
    z = np.sum(p, axis=1, keepdims=True)
    goutq = mxq(f64(gout), 0, "e4m3")
    valsidxg = valsu[:, idx]
    c0 = goutq.T @ valsidxg
    dz = np.sum(c0 * p / np.square(z) * (-1.0), axis=1, keepdims=True)
    dp = c0 / z + dz
    ds0 = dp * 3.0 * (1.0 - f64(share))
    de0 = dp * f64(share)
    da = ds0 * s0 * (1.0 - s0) + de0 * e0
    gs = da * f64(qs)
    qrowsq = mxq(f64(qrows), 0, "e4m3")
    gsq = mxq(gs, 0, "e4m3")
    gk = qrowsq.T @ gsq
    gf = np.zeros((D, U))
    gf[:, idx4] = gk
    y = f64(old) * f64(fade) + gf
    return y

@@ -1,0 +1,273 @@
+from contextlib import ExitStack
+
+import concourse.mybir as mybir
+from concourse.masks import make_identity
+
+D, E, T, I, Q, U = 512, 512, 1024, 256, 512, 1024
+FLOPS = 2 * Q * I * (D + E + D)
+
+F32 = mybir.dt.float32
+BF16 = mybir.dt.bfloat16
+I32 = mybir.dt.int32
+U32 = mybir.dt.uint32
+U16 = mybir.dt.uint16
+U8 = mybir.dt.uint8
+FP8X4 = mybir.dt.float8_e4m3fn_x4
+FP4X4 = mybir.dt.float4_e2m1fn_x4
+ACT = mybir.ActivationFunctionType
+ALU = mybir.AluOpType
+
+P = 128
+PACK = 4
+HALF = 256
+BANK = 512
+
+
+def tile_attend_bmixedparts_k_kernel(tc, query, keys_words, keys_scales, share, gout, vals_words, vals_scales,
+                                      qs, qrows, old, fade, offs, offs4, out):
+    nc = tc.nc
+    with ExitStack() as ctx:
+        lists = ctx.enter_context(tc.tile_pool(name="lists", bufs=1))
+        sb = ctx.enter_context(tc.tile_pool(name="sb", bufs=1))
+        ps = ctx.enter_context(tc.psum_pool(name="ps", bufs=1))
+
+        def bank(b, name):
+            return ps.tile([P, BANK], F32, name=name, tag="bank%d" % b)
+
+        slots = lists.tile([P, I // 16], U16, name="slots")
+        places = lists.tile([P, I // 16], U16, name="places")
+        nc.sync.dma_start(slots[:], offs)
+
+        def load_words(words, name):
+            w = sb.tile([P, T], U16, name=name + "_w", align_bytes=64)
+            nc.sync.dma_start(w[:].bitcast(I32), words[0].bitcast(I32))
+            return w
+
+        def load_scales(scales, queue, name):
+            s = sb.tile([P, T], U8, name=name + "_s", align_bytes=64)
+            for quad in range(4):
+                rows = scales[0, 4 * quad:4 * quad + 4, :].bitcast(I32)
+                queue.dma_start(s[32 * quad:32 * (quad + 1), :].bitcast(I32), rows.unsqueeze(0).to_broadcast([8, 4, T // 4]))
+            return s
+
+        def gather_pool(w, s, name):
+            gw = sb.tile([P, I], U16, name=name + "_gw", align_bytes=64)
+            gs = sb.tile([P, I], U8, name=name + "_gs", align_bytes=64)
+            nc.vector.tensor_copy(gw[:], w[:].indirect(slots[:]))
+            nc.vector.tensor_copy(gs[:], s[:].indirect(slots[:]))
+            return gw, gs
+
+        def load_half(src, h, name):
+            raw = sb.tile([P, PACK, HALF], F32, name="%s_raw%d" % (name, h))
+            nc.sync.dma_start(raw[:], src[:, h * HALF:(h + 1) * HALF].rearrange("(p j) c -> p j c", j=PACK))
+            return raw
+
+        def load_halves(src, name):
+            return [load_half(src, h, name) for h in range(2)]
+
+        def copy_on(engine, dst, src):
+            if engine == "scalar":
+                nc.scalar.activation(dst, src, ACT.Copy)
+            else:
+                nc.vector.tensor_copy(dst, src)
+
+        def deal(halves, on_vector, name):
+            grouped = sb.tile([P, PACK, P, PACK], BF16, name=name + "_bf", align_bytes=64)
+            for h in range(2):
+                src = halves[h][:].rearrange("p j (s r) -> p s j r", r=PACK)
+                dst = grouped[:, :, 64 * h:64 * (h + 1), :].rearrange("p r s j -> p s j r")
+                copy_on("vector", dst[:, 0:on_vector], src[:, 0:on_vector])
+                if on_vector < 64:
+                    copy_on("scalar", dst[:, on_vector:64], src[:, on_vector:64])
+            return grouped[:].rearrange("p r s j -> p (r s j)")
+
+        def quantize(flat, width, calls, name):
+            codes = sb.tile([P, width], U32, name=name + "_codes", align_bytes=64)
+            scales = sb.tile([P, width], U8, name=name + "_scales", align_bytes=64)
+            step = width // calls
+            for c in range(0, width, step):
+                nc.vector.quantize_mx(out=codes[:, c:c + step].bitcast(FP8X4), scales=scales[:, c:c + step],
+                                      in_=flat[:, PACK * c:PACK * (c + step)])
+            return codes, scales
+
+        def scores(stat, moving, first_bank, name):
+            banks = [bank(first_bank + b, "%s%d" % (name, b)) for b in range(2)]
+            tiles = []
+            for r in range(PACK):
+                dst = banks[r // 2][:, (r % 2) * I:(r % 2 + 1) * I]
+                cols = slice(r * P, (r + 1) * P)
+                nc.tensor.matmul_mx(out=dst, lhsT=stat[0][:, cols].bitcast(FP8X4), lhsT_scale=stat[1][:, cols],
+                                    rhs=moving[0], rhs_scale=moving[1], start=True, stop=True)
+                tiles.append(dst)
+            return tiles
+
+        keys = (load_words(keys_words, "keys"), load_scales(keys_scales, nc.sync, "keys"))
+        q_raw = load_halves(query, "query")
+        g_first = load_half(gout, 0, "gout")
+        vals = (load_words(vals_words, "vals"), load_scales(vals_scales, nc.sync, "vals"))
+        g_raw = [g_first, load_half(gout, 1, "gout")]
+        sh = sb.tile([P, PACK], F32, name="sh")
+        nc.sync.dma_start(sh[:], share.rearrange("(p r) o -> p (r o)", r=PACK))
+        rs = sb.tile([P, PACK], F32, name="rs")
+        nc.sync.dma_start(rs[:], qs.rearrange("(p r) o -> p (r o)", r=PACK))
+        r_raw = load_halves(qrows, "qrows")
+        fade_rows = sb.tile([P, P], F32, name="fade_rows")
+        nc.gpsimd.memset(fade_rows[:], 0.0)
+        nc.sync.dma_start(fade_rows[0:U // P, :], fade.rearrange("o (c p) -> (o c) p", p=P))
+        olds = []
+        for j in range(PACK):
+            o = sb.tile([P, U], F32, name="old%d" % j)
+            nc.sync.dma_start(o[:], old[j * P:(j + 1) * P, :])
+            olds.append(o)
+        nc.sync.dma_start(places[:], offs4)
+
+        ident = sb.tile([P, P], F32, name="ident")
+        make_identity(nc, ident[:])
+        windows = [sb.tile([P, U], F32, name="window%d" % w) for w in range(2)]
+        for w in windows:
+            nc.vector.memset(w[:], 0.0)
+
+        b3 = sb.tile([P, PACK], F32, name="b3")
+        nc.vector.tensor_scalar(b3[:], sh[:], -3.0, 3.0, ALU.mult, ALU.add)
+
+        kw, ks = gather_pool(keys[0], keys[1], "keys")
+        q_mx = quantize(deal(q_raw, 40, "query"), Q, 2, "query")
+        a = scores(q_mx, (kw[:].bitcast(FP4X4), ks[:]), 0, "a")
+        vw, vs = gather_pool(vals[0], vals[1], "vals")
+
+        e0 = sb.tile([P, PACK, I], F32, name="e0")
+        s0 = sb.tile([P, PACK, I], F32, name="s0")
+        esum = sb.tile([P, PACK], F32, name="esum")
+        ssum = sb.tile([P, PACK], F32, name="ssum")
+        for r in range(PACK):
+            nc.scalar.activation(e0[:, r, :], a[r], ACT.Exp, accum_out=esum[:, r:r + 1])
+        for r in range(PACK):
+            nc.scalar.activation(s0[:, r, :], a[r], ACT.Sigmoid, accum_out=ssum[:, r:r + 1])
+
+        g_mx = quantize(deal(g_raw, 64, "gout"), Q, 2, "gout")
+        c0 = scores(g_mx, (vw[:].bitcast(FP4X4), vs[:]), 2, "c")
+
+        cq = sb.tile([P, 2, PACK], F32, name="cq")
+        nc.vector.tensor_tensor(cq[:, 0, :], sh[:], rs[:], ALU.mult)
+        nc.vector.scalar_tensor_tensor(cq[:, 1, :], b3[:], -1.0, rs[:], ALU.mult, ALU.mult)
+        ze = sb.tile([P, PACK], F32, name="ze")
+        nc.vector.tensor_tensor(ze[:], esum[:], sh[:], ALU.mult)
+
+        prods = [sb.tile([P, I], F32, name="prod%d" % k) for k in range(2)]
+        ce = sb.tile([P, PACK], F32, name="ce")
+        cs = sb.tile([P, PACK], F32, name="cs")
+        for r in range(PACK):
+            nc.vector.scalar_tensor_tensor(prods[r % 2][:], e0[:, r, :], sh[:, r:r + 1], c0[r], ALU.mult, ALU.mult,
+                                           accum_out=ce[:, r:r + 1])
+
+        def x_op(r):
+            nc.vector.scalar_tensor_tensor(prods[r % 2][:], s0[:, r, :], b3[:, r:r + 1], c0[r], ALU.mult, ALU.mult,
+                                           accum_out=cs[:, r:r + 1])
+
+        slope = sb.tile([P, PACK, I], F32, name="slope")
+
+        def u_op(h):
+            v = s0[:, 2 * h:2 * h + 2, :]
+            nc.vector.scalar_tensor_tensor(slope[:, 2 * h:2 * h + 2, :], v, 1.0, v, ALU.subtract, ALU.mult)
+
+        zs = sb.tile([P, PACK], F32, name="zs")
+        z = sb.tile([P, PACK], F32, name="z")
+        rz = sb.tile([P, PACK], F32, name="rz")
+        kk = sb.tile([P, 2, PACK], F32, name="kk")
+        cp = sb.tile([P, PACK], F32, name="cp")
+        mean = sb.tile([P, PACK], F32, name="mean")
+        x_op(0)
+        x_op(1)
+        nc.vector.tensor_tensor(zs[:], ssum[:], b3[:], ALU.mult)
+        x_op(2)
+        nc.vector.tensor_tensor(z[:], zs[:], ze[:], ALU.add)
+        x_op(3)
+        nc.vector.reciprocal(rz[:], z[:])
+        u_op(0)
+        nc.vector.tensor_tensor(kk[:], cq[:], rz[:].unsqueeze(1).to_broadcast([P, 2, PACK]), ALU.mult)
+        nc.vector.tensor_tensor(cp[:], cs[:], ce[:], ALU.add)
+        u_op(1)
+        nc.vector.tensor_tensor(mean[:], cp[:], rz[:], ALU.mult)
+
+        ek = sb.tile([P, PACK, I], F32, name="ek")
+        hk = sb.tile([P, PACK, I], F32, name="hk")
+        gs = sb.tile([P, PACK, I], BF16, name="gs")
+        for r in range(PACK):
+            nc.scalar.activation(ek[:, r, :], e0[:, r, :], ACT.Copy, scale=kk[:, 0, r:r + 1])
+
+        def h_op(r):
+            nc.vector.scalar_tensor_tensor(hk[:, r, :], slope[:, r, :], kk[:, 1, r:r + 1], ek[:, r, :], ALU.mult, ALU.add)
+
+        def g_op(r):
+            nc.vector.scalar_tensor_tensor(gs[:, r, :], c0[r], mean[:, r:r + 1], hk[:, r, :], ALU.subtract, ALU.mult)
+
+        h_op(0)
+        for r in range(1, PACK):
+            h_op(r)
+            g_op(r - 1)
+        g_op(PACK - 1)
+
+        rows_bf = sb.tile([P, D, PACK], BF16, name="rows_bf", align_bytes=64)
+        for h in range(2):
+            nc.scalar.copy(rows_bf[:, h * HALF:(h + 1) * HALF, :].rearrange("p (c i) t -> p c t i", i=4),
+                           r_raw[h][:].rearrange("p t (c i) -> p c t i", i=4))
+        gs_words = sb.tile([P, I, PACK], BF16, name="gs_words", align_bytes=64)
+        weave_dst = gs_words[:].rearrange("p (c i) t -> p c t i", i=4)
+        weave_src = gs[:].rearrange("p t (c i) -> p c t i", i=4)
+        nc.vector.tensor_copy(weave_dst[:, 0:44], weave_src[:, 0:44])
+        nc.scalar.copy(weave_dst[:, 44:64], weave_src[:, 44:64])
+        r_mx = quantize(rows_bf[:].rearrange("p d t -> p (d t)"), D, 2, "qrows")
+        gs_mx = quantize(gs_words[:].rearrange("p i t -> p (i t)"), I, 1, "gs")
+        gk_ps = scores(r_mx, (gs_mx[0][:].bitcast(FP8X4), gs_mx[1][:]), 0, "gk")
+        gk = []
+        for j in range(PACK):
+            g = sb.tile([P, I], F32, name="gk%d" % j)
+            nc.scalar.copy(g[:], gk_ps[j])
+            gk.append(g)
+
+        fade_ps = bank(7, "fade_ps")
+        nc.tensor.transpose(fade_ps[:, 0:P], fade_rows[:], ident[:])
+        fade_col = sb.tile([P, U // P], F32, name="fade_col")
+        nc.scalar.copy(fade_col[:], fade_ps[:, 0:U // P])
+        turned = []
+        for g in range(2):
+            ft = sb.tile([P, U // P, 2, P], F32, name="turned%d" % g)
+            for cc in range(U // P // 2):
+                t_ps = bank(4 + cc % 2, "old_t%d_%d" % (g, cc))
+                for k in range(2):
+                    c = 2 * cc + k
+                    for jj in range(2):
+                        at = (2 * k + jj) * P
+                        nc.tensor.transpose(t_ps[:, at:at + P], olds[2 * g + jj][:, c * P:(c + 1) * P], ident[:])
+                for k in range(2):
+                    c = 2 * cc + k
+                    nc.scalar.activation(ft[:, c, :, :].rearrange("p j d -> p (j d)"), t_ps[:, 2 * k * P:2 * (k + 1) * P],
+                                         ACT.Copy, scale=fade_col[:, c:c + 1])
+            turned.append(ft)
+
+        first_banks = (6, 2, 0, 4)
+        faded = []
+        for j in range(PACK):
+            halves = []
+            for h in range(2):
+                f_ps = bank(first_banks[j] + h, "faded%d_%d" % (j, h))
+                for k in range(4):
+                    nc.tensor.transpose(f_ps[:, k * P:(k + 1) * P], turned[j // 2][:, 4 * h + k, j % 2, :], ident[:])
+                halves.append(f_ps)
+            faded.append(halves)
+
+        def scatter(j):
+            nc.vector.tensor_copy(windows[j % 2][:].indirect(places[:]), gk[j][:])
+
+        def finish(j):
+            for h in range(2):
+                y = sb.tile([P, BANK], F32, name="y%d_%d" % (j, h))
+                cols = slice(h * BANK, (h + 1) * BANK)
+                nc.vector.tensor_tensor(y[:], faded[j][h][:], windows[j % 2][:, cols], ALU.add)
+                nc.sync.dma_start(out[j * P:(j + 1) * P, cols], y[:])
+
+        scatter(0)
+        for j in range(1, PACK):
+            scatter(j)
+            finish(j - 1)
+        finish(PACK - 1)

@@ -43,11 +43,11 @@ def tile_attend_bmixedparts_k_kernel(tc, query, keys_words, keys_scales, share, 
             nc.sync.dma_start(w[:].bitcast(I32), words[0].bitcast(I32))
             return w
 
-        def load_scales(scales, queue, name):
+        def load_scales(scales, name):
             s = sb.tile([P, T], U8, name=name + "_s", align_bytes=64)
             for quad in range(4):
                 rows = scales[0, 4 * quad:4 * quad + 4, :].bitcast(I32)
-                queue.dma_start(s[32 * quad:32 * (quad + 1), :].bitcast(I32), rows.unsqueeze(0).to_broadcast([8, 4, T // 4]))
+                nc.sync.dma_start(s[32 * quad:32 * (quad + 1), :].bitcast(I32), rows.unsqueeze(0).to_broadcast([8, 4, T // 4]))
             return s
 
         def gather_pool(w, s, name):
@@ -58,7 +58,7 @@ def tile_attend_bmixedparts_k_kernel(tc, query, keys_words, keys_scales, share, 
             return gw, gs
 
         def load_half(src, h, name):
-            raw = sb.tile([P, PACK, HALF], F32, name="%s_raw%d" % (name, h))
+            raw = sb.tile([P, PACK, HALF], F32, name="%s_raw%d" % (name, h), tag="%s_raw%d" % (name, h))
             nc.sync.dma_start(raw[:], src[:, h * HALF:(h + 1) * HALF].rearrange("(p j) c -> p j c", j=PACK))
             return raw
 
@@ -72,7 +72,7 @@ def tile_attend_bmixedparts_k_kernel(tc, query, keys_words, keys_scales, share, 
                 nc.vector.tensor_copy(dst, src)
 
         def deal(halves, on_vector, name):
-            grouped = sb.tile([P, PACK, P, PACK], BF16, name=name + "_bf", align_bytes=64)
+            grouped = sb.tile([P, PACK, P, PACK], BF16, name=name + "_bf", tag=name + "_bf", align_bytes=64)
             for h in range(2):
                 src = halves[h][:].rearrange("p j (s r) -> p s j r", r=PACK)
                 dst = grouped[:, :, 64 * h:64 * (h + 1), :].rearrange("p r s j -> p s j r")
@@ -101,34 +101,33 @@ def tile_attend_bmixedparts_k_kernel(tc, query, keys_words, keys_scales, share, 
                 tiles.append(dst)
             return tiles
 
-        keys = (load_words(keys_words, "keys"), load_scales(keys_scales, nc.sync, "keys"))
+        keys = (load_words(keys_words, "keys"), load_scales(keys_scales, "keys"))
         q_raw = load_halves(query, "query")
         g_first = load_half(gout, 0, "gout")
-        vals = (load_words(vals_words, "vals"), load_scales(vals_scales, nc.sync, "vals"))
+        vals = (load_words(vals_words, "vals"), load_scales(vals_scales, "vals"))
         g_raw = [g_first, load_half(gout, 1, "gout")]
         sh = sb.tile([P, PACK], F32, name="sh")
-        nc.sync.dma_start(sh[:], share.rearrange("(p r) o -> p (r o)", r=PACK))
+        nc.gpsimd.dma_start(sh[:], share.rearrange("(p r) o -> p (r o)", r=PACK))
         rs = sb.tile([P, PACK], F32, name="rs")
-        nc.sync.dma_start(rs[:], qs.rearrange("(p r) o -> p (r o)", r=PACK))
-        r_raw = load_halves(qrows, "qrows")
+        nc.gpsimd.dma_start(rs[:], qs.rearrange("(p r) o -> p (r o)", r=PACK))
+        r_raw = sb.tile([P, PACK, D], F32, name="qrows_raw")
+        nc.sync.dma_start(r_raw[:], qrows.rearrange("(p t) d -> p t d", t=PACK))
         fade_rows = sb.tile([P, P], F32, name="fade_rows")
         nc.gpsimd.memset(fade_rows[:], 0.0)
-        nc.sync.dma_start(fade_rows[0:U // P, :], fade.rearrange("o (c p) -> (o c) p", p=P))
+        nc.gpsimd.dma_start(fade_rows[0:U // P, :], fade.rearrange("o (c p) -> (o c) p", p=P))
         olds = []
         for j in range(PACK):
-            o = sb.tile([P, U], F32, name="old%d" % j)
-            nc.sync.dma_start(o[:], old[j * P:(j + 1) * P, :])
+            o = sb.tile([P, PACK, HALF], F32, name="old%d" % j)
+            nc.sync.dma_start(o[:], old[:, j * HALF:(j + 1) * HALF].rearrange("(j p) u -> p j u", p=P))
             olds.append(o)
         nc.sync.dma_start(places[:], offs4)
 
         ident = sb.tile([P, P], F32, name="ident")
         make_identity(nc, ident[:])
-        windows = [sb.tile([P, U], F32, name="window%d" % w) for w in range(2)]
+        windows = [sb.tile([P, U], F32, name="window%d" % w) for w in range(3)]
         for w in windows:
             nc.vector.memset(w[:], 0.0)
 
-        b3 = sb.tile([P, PACK], F32, name="b3")
-        nc.vector.tensor_scalar(b3[:], sh[:], -3.0, 3.0, ALU.mult, ALU.add)
 
         kw, ks = gather_pool(keys[0], keys[1], "keys")
         q_mx = quantize(deal(q_raw, 40, "query"), Q, 2, "query")
@@ -147,7 +146,9 @@ def tile_attend_bmixedparts_k_kernel(tc, query, keys_words, keys_scales, share, 
         g_mx = quantize(deal(g_raw, 64, "gout"), Q, 2, "gout")
         c0 = scores(g_mx, (vw[:].bitcast(FP4X4), vs[:]), 2, "c")
 
-        cq = sb.tile([P, 2, PACK], F32, name="cq")
+        b3 = sb.tile([P, PACK], F32, name="b3", tag="query_bf", align_bytes=64)
+        nc.vector.tensor_scalar(b3[:], sh[:], -3.0, 3.0, ALU.mult, ALU.add)
+        cq = sb.tile([P, 2, PACK], F32, name="cq", tag="query_raw1")
         nc.vector.tensor_tensor(cq[:, 0, :], sh[:], rs[:], ALU.mult)
         nc.vector.scalar_tensor_tensor(cq[:, 1, :], b3[:], -1.0, rs[:], ALU.mult, ALU.mult)
         ze = sb.tile([P, PACK], F32, name="ze")
@@ -170,28 +171,26 @@ def tile_attend_bmixedparts_k_kernel(tc, query, keys_words, keys_scales, share, 
             v = s0[:, 2 * h:2 * h + 2, :]
             nc.vector.scalar_tensor_tensor(slope[:, 2 * h:2 * h + 2, :], v, 1.0, v, ALU.subtract, ALU.mult)
 
-        zs = sb.tile([P, PACK], F32, name="zs")
         z = sb.tile([P, PACK], F32, name="z")
         rz = sb.tile([P, PACK], F32, name="rz")
         kk = sb.tile([P, 2, PACK], F32, name="kk")
         cp = sb.tile([P, PACK], F32, name="cp")
         mean = sb.tile([P, PACK], F32, name="mean")
-        x_op(0)
-        x_op(1)
-        nc.vector.tensor_tensor(zs[:], ssum[:], b3[:], ALU.mult)
-        x_op(2)
-        nc.vector.tensor_tensor(z[:], zs[:], ze[:], ALU.add)
-        x_op(3)
+        for r in range(PACK):
+            nc.scalar.activation(z[:, r:r + 1], ssum[:, r:r + 1], ACT.Identity, bias=ze[:, r:r + 1], scale=b3[:, r:r + 1])
         nc.vector.reciprocal(rz[:], z[:])
+        for r in range(PACK):
+            nc.scalar.activation(kk[:, :, r], cq[:, :, r], ACT.Copy, scale=rz[:, r:r + 1])
+        for r in range(PACK):
+            x_op(r)
         u_op(0)
-        nc.vector.tensor_tensor(kk[:], cq[:], rz[:].unsqueeze(1).to_broadcast([P, 2, PACK]), ALU.mult)
         nc.vector.tensor_tensor(cp[:], cs[:], ce[:], ALU.add)
         u_op(1)
         nc.vector.tensor_tensor(mean[:], cp[:], rz[:], ALU.mult)
 
         ek = sb.tile([P, PACK, I], F32, name="ek")
         hk = sb.tile([P, PACK, I], F32, name="hk")
-        gs = sb.tile([P, PACK, I], BF16, name="gs")
+        gs = sb.tile([P, PACK, I], BF16, name="gs", tag="gs", align_bytes=64)
         for r in range(PACK):
             nc.scalar.activation(ek[:, r, :], e0[:, r, :], ACT.Copy, scale=kk[:, 0, r:r + 1])
 
@@ -208,66 +207,95 @@ def tile_attend_bmixedparts_k_kernel(tc, query, keys_words, keys_scales, share, 
         g_op(PACK - 1)
 
         rows_bf = sb.tile([P, D, PACK], BF16, name="rows_bf", align_bytes=64)
-        for h in range(2):
-            nc.scalar.copy(rows_bf[:, h * HALF:(h + 1) * HALF, :].rearrange("p (c i) t -> p c t i", i=4),
-                           r_raw[h][:].rearrange("p t (c i) -> p c t i", i=4))
+        for h in range(PACK):
+            cols = slice(h * P, (h + 1) * P)
+            nc.scalar.copy(rows_bf[:, cols, :].rearrange("p (c i) t -> p c t i", i=4),
+                           r_raw[:, :, cols].rearrange("p t (c i) -> p c t i", i=4))
         gs_words = sb.tile([P, I, PACK], BF16, name="gs_words", align_bytes=64)
         weave_dst = gs_words[:].rearrange("p (c i) t -> p c t i", i=4)
         weave_src = gs[:].rearrange("p t (c i) -> p c t i", i=4)
-        nc.vector.tensor_copy(weave_dst[:, 0:44], weave_src[:, 0:44])
-        nc.scalar.copy(weave_dst[:, 44:64], weave_src[:, 44:64])
-        r_mx = quantize(rows_bf[:].rearrange("p d t -> p (d t)"), D, 2, "qrows")
+        nc.vector.tensor_copy(weave_dst, weave_src)
+        rows_flat = rows_bf[:].rearrange("p d t -> p (d t)")
+        r_first = quantize(rows_flat[:, 0:PACK * HALF], HALF, 1, "qrows0")
         gs_mx = quantize(gs_words[:].rearrange("p i t -> p (i t)"), I, 1, "gs")
-        gk_ps = scores(r_mx, (gs_mx[0][:].bitcast(FP8X4), gs_mx[1][:]), 0, "gk")
-        gk = []
-        for j in range(PACK):
-            g = sb.tile([P, I], F32, name="gk%d" % j)
-            nc.scalar.copy(g[:], gk_ps[j])
-            gk.append(g)
-
-        fade_ps = bank(7, "fade_ps")
+        late_codes = sb.tile([P, HALF], U32, name="qrows1_codes", tag="gs", align_bytes=64)
+        late_scales = sb.tile([P, HALF], U8, name="qrows1_scales", align_bytes=64)
+        nc.vector.quantize_mx(out=late_codes[:].bitcast(FP8X4), scales=late_scales[:], in_=rows_flat[:, PACK * HALF:])
+        fade_ps = bank(1, "fade_ps")
         nc.tensor.transpose(fade_ps[:, 0:P], fade_rows[:], ident[:])
         fade_col = sb.tile([P, U // P], F32, name="fade_col")
         nc.scalar.copy(fade_col[:], fade_ps[:, 0:U // P])
         turned = []
-        for g in range(2):
-            ft = sb.tile([P, U // P, 2, P], F32, name="turned%d" % g)
-            for cc in range(U // P // 2):
-                t_ps = bank(4 + cc % 2, "old_t%d_%d" % (g, cc))
-                for k in range(2):
-                    c = 2 * cc + k
-                    for jj in range(2):
-                        at = (2 * k + jj) * P
-                        nc.tensor.transpose(t_ps[:, at:at + P], olds[2 * g + jj][:, c * P:(c + 1) * P], ident[:])
-                for k in range(2):
-                    c = 2 * cc + k
-                    nc.scalar.activation(ft[:, c, :, :].rearrange("p j d -> p (j d)"), t_ps[:, 2 * k * P:2 * (k + 1) * P],
-                                         ACT.Copy, scale=fade_col[:, c:c + 1])
+        for c in range(U // P):
+            t_ps = bank((4, 5, 0, 1)[c % 4], "old_t%d" % c)
+            for j in range(PACK):
+                nc.tensor.transpose(t_ps[:, j * P:(j + 1) * P], olds[c // 2][:, j, (c % 2) * P:(c % 2 + 1) * P], ident[:])
+            ft = sb.tile([P, D], F32, name="turned%d" % c)
+            nc.scalar.activation(ft[:], t_ps[:], ACT.Copy, scale=fade_col[:, c:c + 1])
             turned.append(ft)
 
-        first_banks = (6, 2, 0, 4)
-        faded = []
+        gk = []
+        gk_banks = (2, 3, 0, 1)
         for j in range(PACK):
-            halves = []
-            for h in range(2):
-                f_ps = bank(first_banks[j] + h, "faded%d_%d" % (j, h))
-                for k in range(4):
-                    nc.tensor.transpose(f_ps[:, k * P:(k + 1) * P], turned[j // 2][:, 4 * h + k, j % 2, :], ident[:])
-                halves.append(f_ps)
-            faded.append(halves)
+            codes, scales = (r_first, (late_codes, late_scales))[j // 2]
+            cols = slice((j % 2) * P, (j % 2 + 1) * P)
+            gk_ps = bank(gk_banks[j], "gk%d" % j)
+            nc.tensor.matmul_mx(out=gk_ps[:, 0:I], lhsT=codes[:, cols].bitcast(FP8X4), lhsT_scale=scales[:, cols],
+                                rhs=gs_mx[0][:].bitcast(FP8X4), rhs_scale=gs_mx[1][:], start=True, stop=True)
+            g = sb.tile([P, I], F32, name="gk_sb%d" % j)
+            copy_on("vector" if j == 0 else "scalar", g[:], gk_ps[:, 0:I])
+            gk.append(g)
+
+        window_of = (0, 1, 2, 1)
 
         def scatter(j):
-            nc.vector.tensor_copy(windows[j % 2][:].indirect(places[:]), gk[j][:])
+            nc.vector.tensor_copy(windows[window_of[j]][:].indirect(places[:]), gk[j][:])
 
-        def finish(j):
+        def turn_back(j, h, b):
+            f_ps = bank(b, "faded%d_%d" % (j, h))
+            for k in range(4):
+                nc.tensor.transpose(f_ps[:, k * P:(k + 1) * P], turned[4 * h + k][:, j * P:(j + 1) * P], ident[:])
+            return f_ps
+
+        def add_on_vector(j, h, f_ps):
+            y = sb.tile([P, BANK], F32, name="y%d_%d" % (j, h))
+            cols = slice(h * BANK, (h + 1) * BANK)
+            nc.vector.tensor_tensor(y[:], f_ps[:], windows[window_of[j]][:, cols], ALU.add)
+            nc.sync.dma_start(out[j * P:(j + 1) * P, cols], y[:])
+
+        def turn_window(h):
+            w_ps = bank(4 + h, "window_t%d" % h)
+            for k in range(4):
+                at = h * BANK + k * P
+                nc.tensor.transpose(w_ps[:, k * P:(k + 1) * P], windows[0][:, at:at + P], ident[:])
+            w_sb = sb.tile([P, BANK], F32, name="window_turned%d" % h)
+            nc.scalar.copy(w_sb[:], w_ps[:])
+            return w_sb
+
+        def add_on_tensor(h, w_sb):
+            y_ps = bank(6 + h, "sum0_%d" % h)
+            for k in range(4):
+                dst = y_ps[:, k * P:(k + 1) * P]
+                nc.tensor.matmul(dst, turned[4 * h + k][:, 0:P], ident[:], start=True, stop=False, is_transpose=True)
+                nc.tensor.matmul(dst, w_sb[:, k * P:(k + 1) * P], ident[:], start=False, stop=True, is_transpose=True)
+            y = sb.tile([P, BANK], F32, name="y0_%d" % h)
+            nc.scalar.copy(y[:], y_ps[:])
+            nc.scalar.dma_start(out[0:P, h * BANK:(h + 1) * BANK], y[:])
+
+        faded = {}
+        for j in (1, 2):
             for h in range(2):
-                y = sb.tile([P, BANK], F32, name="y%d_%d" % (j, h))
-                cols = slice(h * BANK, (h + 1) * BANK)
-                nc.vector.tensor_tensor(y[:], faded[j][h][:], windows[j % 2][:, cols], ALU.add)
-                nc.sync.dma_start(out[j * P:(j + 1) * P, cols], y[:])
-
+                faded[(j, h)] = turn_back(j, h, gk_banks[2 * (j - 1) + h])
         scatter(0)
-        for j in range(1, PACK):
+        window_turned = [turn_window(h) for h in range(2)]
+        for h in range(2):
+            faded[(3, h)] = turn_back(3, h, 4 + h)
+        for h in range(2):
+            add_on_tensor(h, window_turned[h])
+        scatter(1)
+        for j in (2, 3):
             scatter(j)
-            finish(j - 1)
-        finish(PACK - 1)
+            for h in range(2):
+                add_on_vector(j - 1, h, faded[(j - 1, h)])
+        for h in range(2):
+            add_on_vector(3, h, faded[(3, h)])

@@ -45,9 +45,9 @@ def tile_attend_bmixedparts_k_kernel(tc, query, keys_words, keys_scales, share, 
 
         def load_scales(scales, name):
             s = sb.tile([P, T], U8, name=name + "_s", align_bytes=64)
+            nc.gpsimd.memset(s[:].bitcast(I32), 0)
             for quad in range(4):
-                rows = scales[0, 4 * quad:4 * quad + 4, :].bitcast(I32)
-                nc.sync.dma_start(s[32 * quad:32 * (quad + 1), :].bitcast(I32), rows.unsqueeze(0).to_broadcast([8, 4, T // 4]))
+                nc.sync.dma_start(s[32 * quad:32 * quad + 4, :].bitcast(I32), scales[0, 4 * quad:4 * quad + 4, :].bitcast(I32))
             return s
 
         def gather_pool(w, s, name):
@@ -74,8 +74,8 @@ def tile_attend_bmixedparts_k_kernel(tc, query, keys_words, keys_scales, share, 
         def deal(halves, on_vector, name):
             grouped = sb.tile([P, PACK, P, PACK], BF16, name=name + "_bf", tag=name + "_bf", align_bytes=64)
             for h in range(2):
-                src = halves[h][:].rearrange("p j (s r) -> p s j r", r=PACK)
-                dst = grouped[:, :, 64 * h:64 * (h + 1), :].rearrange("p r s j -> p s j r")
+                src = halves[h][:].rearrange("p j (s r) -> p s r j", r=PACK)
+                dst = grouped[:, :, 64 * h:64 * (h + 1), :].rearrange("p r s j -> p s r j")
                 copy_on("vector", dst[:, 0:on_vector], src[:, 0:on_vector])
                 if on_vector < 64:
                     copy_on("scalar", dst[:, on_vector:64], src[:, on_vector:64])

from contextlib import ExitStack

import concourse.mybir as mybir
from concourse.masks import make_identity

D, E, T, I, Q, U = 512, 512, 1024, 256, 512, 1024
FLOPS = 2 * Q * I * (D + E + D)

F32 = mybir.dt.float32
BF16 = mybir.dt.bfloat16
I32 = mybir.dt.int32
U32 = mybir.dt.uint32
U16 = mybir.dt.uint16
U8 = mybir.dt.uint8
FP8X4 = mybir.dt.float8_e4m3fn_x4
FP4X4 = mybir.dt.float4_e2m1fn_x4
ACT = mybir.ActivationFunctionType
ALU = mybir.AluOpType

P = 128
PACK = 4
HALF = 256
BANK = 512


def tile_attend_bmixedparts_k_kernel(tc, query, keys_words, keys_scales, share, gout, vals_words, vals_scales,
                                      qs, qrows, old, fade, offs, offs4, out):
    nc = tc.nc
    with ExitStack() as ctx:
        lists = ctx.enter_context(tc.tile_pool(name="lists", bufs=1))
        sb = ctx.enter_context(tc.tile_pool(name="sb", bufs=1))
        ps = ctx.enter_context(tc.psum_pool(name="ps", bufs=1))

        def bank(b, name):
            return ps.tile([P, BANK], F32, name=name, tag="bank%d" % b)

        slots = lists.tile([P, I // 16], U16, name="slots")
        places = lists.tile([P, I // 16], U16, name="places")
        nc.sync.dma_start(slots[:], offs)

        def load_words(words, name):
            w = sb.tile([P, T], U16, name=name + "_w", align_bytes=64)
            nc.sync.dma_start(w[:].bitcast(I32), words[0].bitcast(I32))
            return w

        def load_scales(scales, name):
            s = sb.tile([P, T], U8, name=name + "_s", align_bytes=64)
            nc.gpsimd.memset(s[:].bitcast(I32), 0)
            for quad in range(4):
                nc.sync.dma_start(s[32 * quad:32 * quad + 4, :].bitcast(I32), scales[0, 4 * quad:4 * quad + 4, :].bitcast(I32))
            return s

        def gather_pool(w, s, name):
            gw = sb.tile([P, I], U16, name=name + "_gw", align_bytes=64)
            gs = sb.tile([P, I], U8, name=name + "_gs", align_bytes=64)
            nc.vector.tensor_copy(gw[:], w[:].indirect(slots[:]))
            nc.vector.tensor_copy(gs[:], s[:].indirect(slots[:]))
            return gw, gs

        def load_half(src, h, name):
            raw = sb.tile([P, PACK, HALF], F32, name="%s_raw%d" % (name, h), tag="%s_raw%d" % (name, h))
            nc.sync.dma_start(raw[:], src[:, h * HALF:(h + 1) * HALF].rearrange("(p j) c -> p j c", j=PACK))
            return raw

        def load_halves(src, name):
            return [load_half(src, h, name) for h in range(2)]

        def copy_on(engine, dst, src):
            if engine == "scalar":
                nc.scalar.activation(dst, src, ACT.Copy)
            else:
                nc.vector.tensor_copy(dst, src)

        def deal(halves, on_vector, name):
            grouped = sb.tile([P, PACK, P, PACK], BF16, name=name + "_bf", tag=name + "_bf", align_bytes=64)
            for h in range(2):
                src = halves[h][:].rearrange("p j (s r) -> p s r j", r=PACK)
                dst = grouped[:, :, 64 * h:64 * (h + 1), :].rearrange("p r s j -> p s r j")
                copy_on("vector", dst[:, 0:on_vector], src[:, 0:on_vector])
                if on_vector < 64:
                    copy_on("scalar", dst[:, on_vector:64], src[:, on_vector:64])
            return grouped[:].rearrange("p r s j -> p (r s j)")

        def quantize(flat, width, calls, name):
            codes = sb.tile([P, width], U32, name=name + "_codes", align_bytes=64)
            scales = sb.tile([P, width], U8, name=name + "_scales", align_bytes=64)
            step = width // calls
            for c in range(0, width, step):
                nc.vector.quantize_mx(out=codes[:, c:c + step].bitcast(FP8X4), scales=scales[:, c:c + step],
                                      in_=flat[:, PACK * c:PACK * (c + step)])
            return codes, scales

        def scores(stat, moving, first_bank, name):
            banks = [bank(first_bank + b, "%s%d" % (name, b)) for b in range(2)]
            tiles = []
            for r in range(PACK):
                dst = banks[r // 2][:, (r % 2) * I:(r % 2 + 1) * I]
                cols = slice(r * P, (r + 1) * P)
                nc.tensor.matmul_mx(out=dst, lhsT=stat[0][:, cols].bitcast(FP8X4), lhsT_scale=stat[1][:, cols],
                                    rhs=moving[0], rhs_scale=moving[1], start=True, stop=True)
                tiles.append(dst)
            return tiles

        keys = (load_words(keys_words, "keys"), load_scales(keys_scales, "keys"))
        q_raw = load_halves(query, "query")
        g_first = load_half(gout, 0, "gout")
        vals = (load_words(vals_words, "vals"), load_scales(vals_scales, "vals"))
        g_raw = [g_first, load_half(gout, 1, "gout")]
        sh = sb.tile([P, PACK], F32, name="sh")
        nc.gpsimd.dma_start(sh[:], share.rearrange("(p r) o -> p (r o)", r=PACK))
        rs = sb.tile([P, PACK], F32, name="rs")
        nc.gpsimd.dma_start(rs[:], qs.rearrange("(p r) o -> p (r o)", r=PACK))
        r_raw = sb.tile([P, PACK, D], F32, name="qrows_raw")
        nc.sync.dma_start(r_raw[:], qrows.rearrange("(p t) d -> p t d", t=PACK))
        fade_rows = sb.tile([P, P], F32, name="fade_rows")
        nc.gpsimd.memset(fade_rows[:], 0.0)
        nc.gpsimd.dma_start(fade_rows[0:U // P, :], fade.rearrange("o (c p) -> (o c) p", p=P))
        olds = []
        for j in range(PACK):
            o = sb.tile([P, PACK, HALF], F32, name="old%d" % j)
            nc.sync.dma_start(o[:], old[:, j * HALF:(j + 1) * HALF].rearrange("(j p) u -> p j u", p=P))
            olds.append(o)
        nc.sync.dma_start(places[:], offs4)

        ident = sb.tile([P, P], F32, name="ident")
        make_identity(nc, ident[:])
        windows = [sb.tile([P, U], F32, name="window%d" % w) for w in range(3)]
        for w in windows:
            nc.vector.memset(w[:], 0.0)


        kw, ks = gather_pool(keys[0], keys[1], "keys")
        q_mx = quantize(deal(q_raw, 40, "query"), Q, 2, "query")
        a = scores(q_mx, (kw[:].bitcast(FP4X4), ks[:]), 0, "a")
        vw, vs = gather_pool(vals[0], vals[1], "vals")

        e0 = sb.tile([P, PACK, I], F32, name="e0")
        s0 = sb.tile([P, PACK, I], F32, name="s0")
        esum = sb.tile([P, PACK], F32, name="esum")
        ssum = sb.tile([P, PACK], F32, name="ssum")
        for r in range(PACK):
            nc.scalar.activation(e0[:, r, :], a[r], ACT.Exp, accum_out=esum[:, r:r + 1])
        for r in range(PACK):
            nc.scalar.activation(s0[:, r, :], a[r], ACT.Sigmoid, accum_out=ssum[:, r:r + 1])

        g_mx = quantize(deal(g_raw, 64, "gout"), Q, 2, "gout")
        c0 = scores(g_mx, (vw[:].bitcast(FP4X4), vs[:]), 2, "c")

        b3 = sb.tile([P, PACK], F32, name="b3", tag="query_bf", align_bytes=64)
        nc.vector.tensor_scalar(b3[:], sh[:], -3.0, 3.0, ALU.mult, ALU.add)
        cq = sb.tile([P, 2, PACK], F32, name="cq", tag="query_raw1")
        nc.vector.tensor_tensor(cq[:, 0, :], sh[:], rs[:], ALU.mult)
        nc.vector.scalar_tensor_tensor(cq[:, 1, :], b3[:], -1.0, rs[:], ALU.mult, ALU.mult)
        ze = sb.tile([P, PACK], F32, name="ze")
        nc.vector.tensor_tensor(ze[:], esum[:], sh[:], ALU.mult)

        prods = [sb.tile([P, I], F32, name="prod%d" % k) for k in range(2)]
        ce = sb.tile([P, PACK], F32, name="ce")
        cs = sb.tile([P, PACK], F32, name="cs")
        for r in range(PACK):
            nc.vector.scalar_tensor_tensor(prods[r % 2][:], e0[:, r, :], sh[:, r:r + 1], c0[r], ALU.mult, ALU.mult,
                                           accum_out=ce[:, r:r + 1])

        def x_op(r):
            nc.vector.scalar_tensor_tensor(prods[r % 2][:], s0[:, r, :], b3[:, r:r + 1], c0[r], ALU.mult, ALU.mult,
                                           accum_out=cs[:, r:r + 1])

        slope = sb.tile([P, PACK, I], F32, name="slope")

        def u_op(h):
            v = s0[:, 2 * h:2 * h + 2, :]
            nc.vector.scalar_tensor_tensor(slope[:, 2 * h:2 * h + 2, :], v, 1.0, v, ALU.subtract, ALU.mult)

        z = sb.tile([P, PACK], F32, name="z")
        rz = sb.tile([P, PACK], F32, name="rz")
        kk = sb.tile([P, 2, PACK], F32, name="kk")
        cp = sb.tile([P, PACK], F32, name="cp")
        mean = sb.tile([P, PACK], F32, name="mean")
        for r in range(PACK):
            nc.scalar.activation(z[:, r:r + 1], ssum[:, r:r + 1], ACT.Identity, bias=ze[:, r:r + 1], scale=b3[:, r:r + 1])
        nc.vector.reciprocal(rz[:], z[:])
        for r in range(PACK):
            nc.scalar.activation(kk[:, :, r], cq[:, :, r], ACT.Copy, scale=rz[:, r:r + 1])
        for r in range(PACK):
            x_op(r)
        u_op(0)
        nc.vector.tensor_tensor(cp[:], cs[:], ce[:], ALU.add)
        u_op(1)
        nc.vector.tensor_tensor(mean[:], cp[:], rz[:], ALU.mult)

        ek = sb.tile([P, PACK, I], F32, name="ek")
        hk = sb.tile([P, PACK, I], F32, name="hk")
        gs = sb.tile([P, PACK, I], BF16, name="gs", tag="gs", align_bytes=64)
        for r in range(PACK):
            nc.scalar.activation(ek[:, r, :], e0[:, r, :], ACT.Copy, scale=kk[:, 0, r:r + 1])

        def h_op(r):
            nc.vector.scalar_tensor_tensor(hk[:, r, :], slope[:, r, :], kk[:, 1, r:r + 1], ek[:, r, :], ALU.mult, ALU.add)

        def g_op(r):
            nc.vector.scalar_tensor_tensor(gs[:, r, :], c0[r], mean[:, r:r + 1], hk[:, r, :], ALU.subtract, ALU.mult)

        h_op(0)
        for r in range(1, PACK):
            h_op(r)
            g_op(r - 1)
        g_op(PACK - 1)

        rows_bf = sb.tile([P, D, PACK], BF16, name="rows_bf", align_bytes=64)
        for h in range(PACK):
            cols = slice(h * P, (h + 1) * P)
            nc.scalar.copy(rows_bf[:, cols, :].rearrange("p (c i) t -> p c t i", i=4),
                           r_raw[:, :, cols].rearrange("p t (c i) -> p c t i", i=4))
        gs_words = sb.tile([P, I, PACK], BF16, name="gs_words", align_bytes=64)
        weave_dst = gs_words[:].rearrange("p (c i) t -> p c t i", i=4)
        weave_src = gs[:].rearrange("p t (c i) -> p c t i", i=4)
        nc.vector.tensor_copy(weave_dst, weave_src)
        rows_flat = rows_bf[:].rearrange("p d t -> p (d t)")
        r_first = quantize(rows_flat[:, 0:PACK * HALF], HALF, 1, "qrows0")
        gs_mx = quantize(gs_words[:].rearrange("p i t -> p (i t)"), I, 1, "gs")
        late_codes = sb.tile([P, HALF], U32, name="qrows1_codes", tag="gs", align_bytes=64)
        late_scales = sb.tile([P, HALF], U8, name="qrows1_scales", align_bytes=64)
        nc.vector.quantize_mx(out=late_codes[:].bitcast(FP8X4), scales=late_scales[:], in_=rows_flat[:, PACK * HALF:])
        fade_ps = bank(1, "fade_ps")
        nc.tensor.transpose(fade_ps[:, 0:P], fade_rows[:], ident[:])
        fade_col = sb.tile([P, U // P], F32, name="fade_col")
        nc.scalar.copy(fade_col[:], fade_ps[:, 0:U // P])
        turned = []
        for c in range(U // P):
            t_ps = bank((4, 5, 0, 1)[c % 4], "old_t%d" % c)
            for j in range(PACK):
                nc.tensor.transpose(t_ps[:, j * P:(j + 1) * P], olds[c // 2][:, j, (c % 2) * P:(c % 2 + 1) * P], ident[:])
            ft = sb.tile([P, D], F32, name="turned%d" % c)
            nc.scalar.activation(ft[:], t_ps[:], ACT.Copy, scale=fade_col[:, c:c + 1])
            turned.append(ft)

        gk = []
        gk_banks = (2, 3, 0, 1)
        for j in range(PACK):
            codes, scales = (r_first, (late_codes, late_scales))[j // 2]
            cols = slice((j % 2) * P, (j % 2 + 1) * P)
            gk_ps = bank(gk_banks[j], "gk%d" % j)
            nc.tensor.matmul_mx(out=gk_ps[:, 0:I], lhsT=codes[:, cols].bitcast(FP8X4), lhsT_scale=scales[:, cols],
                                rhs=gs_mx[0][:].bitcast(FP8X4), rhs_scale=gs_mx[1][:], start=True, stop=True)
            g = sb.tile([P, I], F32, name="gk_sb%d" % j)
            copy_on("vector" if j == 0 else "scalar", g[:], gk_ps[:, 0:I])
            gk.append(g)

        window_of = (0, 1, 2, 1)

        def scatter(j):
            nc.vector.tensor_copy(windows[window_of[j]][:].indirect(places[:]), gk[j][:])

        def turn_back(j, h, b):
            f_ps = bank(b, "faded%d_%d" % (j, h))
            for k in range(4):
                nc.tensor.transpose(f_ps[:, k * P:(k + 1) * P], turned[4 * h + k][:, j * P:(j + 1) * P], ident[:])
            return f_ps

        def add_on_vector(j, h, f_ps):
            y = sb.tile([P, BANK], F32, name="y%d_%d" % (j, h))
            cols = slice(h * BANK, (h + 1) * BANK)
            nc.vector.tensor_tensor(y[:], f_ps[:], windows[window_of[j]][:, cols], ALU.add)
            nc.sync.dma_start(out[j * P:(j + 1) * P, cols], y[:])

        def turn_window(h):
            w_ps = bank(4 + h, "window_t%d" % h)
            for k in range(4):
                at = h * BANK + k * P
                nc.tensor.transpose(w_ps[:, k * P:(k + 1) * P], windows[0][:, at:at + P], ident[:])
            w_sb = sb.tile([P, BANK], F32, name="window_turned%d" % h)
            nc.scalar.copy(w_sb[:], w_ps[:])
            return w_sb

        def add_on_tensor(h, w_sb):
            y_ps = bank(6 + h, "sum0_%d" % h)
            for k in range(4):
                dst = y_ps[:, k * P:(k + 1) * P]
                nc.tensor.matmul(dst, turned[4 * h + k][:, 0:P], ident[:], start=True, stop=False, is_transpose=True)
                nc.tensor.matmul(dst, w_sb[:, k * P:(k + 1) * P], ident[:], start=False, stop=True, is_transpose=True)
            y = sb.tile([P, BANK], F32, name="y0_%d" % h)
            nc.scalar.copy(y[:], y_ps[:])
            nc.scalar.dma_start(out[0:P, h * BANK:(h + 1) * BANK], y[:])

        faded = {}
        for j in (1, 2):
            for h in range(2):
                faded[(j, h)] = turn_back(j, h, gk_banks[2 * (j - 1) + h])
        scatter(0)
        window_turned = [turn_window(h) for h in range(2)]
        for h in range(2):
            faded[(3, h)] = turn_back(3, h, 4 + h)
        for h in range(2):
            add_on_tensor(h, window_turned[h])
        scatter(1)
        for j in (2, 3):
            scatter(j)
            for h in range(2):
                add_on_vector(j - 1, h, faded[(j - 1, h)])
        for h in range(2):
            add_on_vector(3, h, faded[(3, h)])
